import numpy as np
import ml_dtypes


def mxq(x, axis, fmt="e4m3"):
    dtype, down = {"e4m3": (ml_dtypes.float8_e4m3fn, 7), "e5m2": (ml_dtypes.float8_e5m2, 14)}[fmt]
    v = np.moveaxis(np.asarray(x, np.float32).astype(ml_dtypes.bfloat16).astype(np.float64), axis, -1)
    blocks = v.reshape(v.shape[:-1] + (-1, 32))
    amax = np.abs(blocks).max(-1, keepdims=True)
    byte = np.maximum(np.where(amax > 0, np.frexp(amax)[1] - 1 + 127, 0) - down, 1)
    scale = np.exp2(byte - 127.0)
    codes = (blocks / scale).astype(np.float32).astype(dtype).astype(np.float64)
    return np.moveaxis((codes * scale).reshape(v.shape), -1, axis)


WIDE = False


def mx_kscale(k):
    if not WIDE:
        return np.ones(k)
    levels = np.array([10, -10, 5, -5, 0])
    if k % 512:
        return np.exp2(np.random.permutation(np.resize(levels, k // 32))).repeat(32)
    a = np.empty((k // 512, 16))
    for p in range(k // 512):
        a[p, :8] = np.random.permutation(np.resize(levels, 8))
        for g in range(8):
            far = levels[np.abs(levels - a[p, g]) >= 10]
            a[p, g + 8] = far[np.random.randint(len(far))]
    return np.exp2(a.ravel()).repeat(32)


def f64(x):
    return np.asarray(x).astype(np.float64)


def striped(idx):
    return np.tile(idx.reshape(-1, 16).T, (8, 1)).astype(np.uint16)


def unstriped(offs):
    return offs[:16].T.reshape(-1).astype(np.int64)


def striped8(idx):
    return np.concatenate([x.reshape(-1, 16).T for x in idx]).astype(np.uint16)


def runs(offs, k):
    lists = np.stack([offs[16 * r : 16 * r + 16].T.reshape(-1) for r in range(8)]).astype(np.int64)
    return lists[np.arange(k) % 512 // 64]


def pack_weight(w):
    k, n = w.shape
    w = f64(np.asarray(w, np.float32).astype(ml_dtypes.bfloat16)).reshape(k // 32, 32, n)
    amax = np.abs(w).max(1)
    byte = np.clip(np.where(amax > 0, np.frexp(amax)[1] - 1 + 127 - 7, 1), 1, 254)
    scaled = (w * np.exp2(127.0 - byte)[:, None, :]).reshape(k, n).astype(np.float32)
    words = np.ascontiguousarray(scaled.reshape(k // 512, 128, 4, n).transpose(0, 1, 3, 2)).astype(ml_dtypes.float8_e4m3fn).view(np.uint8)
    return words, np.ascontiguousarray(byte.astype(np.uint8).reshape(k // 512, 16, n))


def unpack_weight(words, scales):
    g, p, n, _ = words.shape
    vals = np.ascontiguousarray(words).view(ml_dtypes.float8_e4m3fn).astype(np.float64) * np.repeat(np.exp2(scales.astype(np.float64) - 127.0), 8, axis=1)[..., None]
    return vals.transpose(0, 1, 3, 2).reshape(g * 512, n)


def sigmoid(v):
    return 1.0 / (1.0 + np.exp(-np.maximum(v, -700.0)))

def planes(y):
    n, m = y.shape
    v = y.astype(np.float32).astype(ml_dtypes.bfloat16).astype(np.float64).reshape(n // 32, 32, m)
    top = np.abs(v).max(1)
    byte = np.clip(np.where(top > 0, np.frexp(top)[1] - 1 + 127 - 7, 1), 1, 254)
    codes = (v * np.exp2(127.0 - byte)[:, None, :]).reshape(n, m).astype(np.float32).astype(ml_dtypes.float8_e4m3fn).view(np.uint8)
    words = codes.reshape(n // 512, 128, 4, m).transpose(0, 1, 3, 2)
    return np.ascontiguousarray(words), np.ascontiguousarray(byte.astype(np.uint8).reshape(n // 512, 16, m))


K, T, S, N, G, H, W = 512, 2048, 256, 512, 2048, 512, 128


def setup_inputs():
    n = np.random.standard_normal
    s = mx_kscale(K)[:, None]
    u = mx_kscale(K)
    packed_xT = pack_weight(n((K, T)) * s)
    packed_dT = pack_weight(n((K, G)) / s)
    packed_w1 = pack_weight(n((H, N)) / np.sqrt(H) / u[:, None])
    perm = np.random.permutation(S)
    return {
        "x_words": packed_xT[0],
        "x_scales": packed_xT[1],
        "d_words": packed_dT[0],
        "d_scales": packed_dT[1],
        "gn": (np.random.uniform(0.5, 1.5, (H, 1)) * u[:, None]).astype(np.float32),
        "w1_words": packed_w1[0],
        "w1_scales": packed_w1[1],
        "offs": striped(np.random.permutation(T)[:S]),
        "k1": striped8(np.random.randint(0, G, (8, H))),
        "two": striped(np.random.permutation(T)[:S]),
        "n1": striped8(np.stack([np.random.permutation(S) for _ in range(8)])),
        "n2": striped8(np.stack([np.random.permutation(S) for _ in range(8)])),
        "n3": striped(perm[:W]),
        "n4": striped(perm[W:]),
    }


def reference(x_words, x_scales, d_words, d_scales, gn, w1_words, w1_scales, offs, k1, two, n1, n2, n3, n4):
    d_k1 = unpack_weight(d_words, d_scales)[np.arange(K)[:, None], runs(k1, K)]
    xq = unpack_weight(x_words, x_scales)[:, unstriped(offs)]
    a = 0.0625 * (d_k1.T @ xq)
    x_two = unpack_weight(x_words, x_scales)[:, unstriped(two)]
    b = 0.0625 * (d_k1.T @ x_two)
    z = f64(gn) * ((a + a[np.arange(H)[:, None], runs(n1, H)]) * (sigmoid(b + b[np.arange(H)[:, None], runs(n2, H)])))
    h = unpack_weight(w1_words, w1_scales).T @ mxq(z, 0, "e4m3")
    pa = h[:, unstriped(n3)]
    pb = h[:, unstriped(n4)]
    rb = pa - pb
    ra = 0.75 * (pa + pb)
    ds = np.zeros((N, S))
    ds[:, unstriped(n3)] = ra
    out = ds.copy()
    out[:, unstriped(n4)] = rb
    return (out,) + planes(out)

@@ -1,0 +1,177 @@
+from contextlib import ExitStack
+
+import concourse.mybir as mybir
+
+K, T, S, N, G, H, W = 512, 2048, 256, 512, 2048, 512, 128
+FLOPS = 2 * K * H * S * 2 + 2 * H * N * S
+
+F32 = mybir.dt.float32
+BF16 = mybir.dt.bfloat16
+I32 = mybir.dt.int32
+U32 = mybir.dt.uint32
+U16 = mybir.dt.uint16
+U8 = mybir.dt.uint8
+FP8X4 = mybir.dt.float8_e4m3fn_x4
+ACT = mybir.ActivationFunctionType
+ALU = mybir.AluOpType
+
+P = 128
+PACK = 4
+HALF = 128
+PIECES = ((0, 128), (128, 192), (192, 256))
+
+
+def tile_picked_twkstriebhaar_none_po_kernel(tc, x_words, x_scales, d_words, d_scales, gn, w1_words, w1_scales, offs, k1, two, n1, n2, n3, n4, out_0, out_1, out_2):
+    nc = tc.nc
+    with ExitStack() as ctx:
+        sb = ctx.enter_context(tc.tile_pool(name="sb", bufs=1))
+        ps = ctx.enter_context(tc.psum_pool(name="ps", bufs=1))
+
+        def words_of(ap):
+            return ap[0].rearrange("p n t -> p (n t)").bitcast(I32)
+
+        def load_list(name, ap):
+            tile = sb.tile(list(ap.shape), U16, name=name)
+            nc.sync.dma_start(tile[:], ap)
+            return tile
+
+        d_bytes = sb.tile([P, G], U8, name="d_bytes", align_bytes=64)
+        x_bytes = sb.tile([P, T], U8, name="x_bytes", align_bytes=64)
+        nc.gpsimd.memset(d_bytes[:].bitcast(I32), 0)
+        nc.vector.memset(x_bytes[:].bitcast(I32), 0)
+        nc.scalar.dma_start(x_bytes[:].bitcast(I32)[0:P:8, :], x_scales[0].bitcast(I32))
+
+        k1_list = load_list("k1_list", k1)
+        nc.sync.dma_start(d_bytes[:].bitcast(I32)[0:P:8, :], d_scales[0].bitcast(I32))
+        two_list = load_list("two_list", two)
+        offs_list = load_list("offs_list", offs)
+        d_table = sb.tile([P, G], U32, name="d_table", align_bytes=64)
+        x_table = sb.tile([P, T], U32, name="x_table", align_bytes=64)
+        nc.sync.dma_start(d_table[:].bitcast(I32), words_of(d_words))
+        nc.sync.dma_start(x_table[:].bitcast(I32), words_of(x_words))
+        n2_list = load_list("n2_list", n2)
+        n1_list = load_list("n1_list", n1)
+        n3_list = load_list("n3_list", n3)
+        n4_list = load_list("n4_list", n4)
+
+        gain = sb.tile([P, PACK], F32, name="gain")
+        nc.gpsimd.dma_start(gain[:], gn.rearrange("(p t) o -> p (t o)", t=PACK))
+        w_table = sb.tile([P, N], U32, name="w_table", align_bytes=64)
+        nc.gpsimd.dma_start(w_table[:].bitcast(I32), words_of(w1_words))
+        w_bytes = sb.tile([P, N], U8, name="w_bytes", align_bytes=64)
+        nc.gpsimd.memset(w_bytes[:].bitcast(I32), 0)
+        for q in range(4):
+            nc.gpsimd.dma_start(w_bytes[:].bitcast(I32)[32 * q : 32 * q + 4, :], w1_scales[0, 4 * q : 4 * q + 4, :].bitcast(I32))
+        factor = sb.tile([P, PACK], F32, name="factor")
+        nc.gpsimd.tensor_scalar(factor[:], gain[:], 0.0625, 0.0, ALU.mult, ALU.add)
+
+        d_picked_bytes = sb.tile([P, H], U8, name="d_picked_bytes", align_bytes=64)
+        x_picked_bytes = sb.tile([P, 2 * S], U8, name="x_picked_bytes", align_bytes=64)
+        nc.vector.tensor_copy(d_picked_bytes[:], d_bytes[:].indirect(k1_list[:]))
+        nc.vector.tensor_copy(x_picked_bytes[:, 0:S], x_bytes[:].indirect(two_list[:]))
+        nc.vector.tensor_copy(x_picked_bytes[:, S : 2 * S], x_bytes[:].indirect(offs_list[:]))
+        spread = sb.tile([P, H + 2 * S], U8, name="spread", align_bytes=64)
+        scales = sb.tile([P, H + 2 * S], U8, name="scales", align_bytes=64)
+        nc.vector.tensor_copy(spread[:, 0:H].rearrange("p (t m) -> p t m", t=PACK), d_picked_bytes[:].rearrange("p (m t) -> p t m", t=PACK))
+        nc.vector.tensor_copy(spread[:, H : H + 2 * S].bitcast(I32), x_picked_bytes[:].bitcast(I32))
+        for q in range(4):
+            nc.scalar.dma_start(scales[:].bitcast(I32)[32 * q : 32 * q + 4, :], spread[:].bitcast(I32)[32 * q : 32 * q + 32 : 8, :])
+
+        d_picked = sb.tile([P, H], U32, name="d_picked", align_bytes=64)
+        nc.vector.tensor_copy(d_picked[:], d_table[:].indirect(k1_list[:]))
+        keys = sb.tile([P, H], U32, name="keys", align_bytes=64)
+        nc.vector.tensor_copy(keys[:].rearrange("p (t m i) -> p m t i", t=PACK, i=4), d_picked[:].rearrange("p (m i t) -> p m t i", t=PACK, i=4))
+        x_two = sb.tile([P, S], U32, name="x_two", align_bytes=64)
+        nc.vector.tensor_copy(x_two[:], x_table[:].indirect(two_list[:]))
+        x_idx = sb.tile([P, S], U32, name="x_idx", align_bytes=64)
+        nc.vector.tensor_copy(x_idx[:], x_table[:].indirect(offs_list[:]))
+
+        w_dealt = sb.tile([P, N], U32, name="w_dealt", align_bytes=64)
+        nc.scalar.copy(w_dealt[:].rearrange("p (t m i) -> p m t i", t=PACK, i=4), w_table[:].rearrange("p (m i t) -> p m t i", t=PACK, i=4))
+        w_scales = sb.tile([P, N], U8, name="w_scales", align_bytes=64)
+        nc.gpsimd.tensor_copy(w_scales[:].rearrange("p (t m) -> p t m", t=PACK), w_bytes[:].rearrange("p (m t) -> p t m", t=PACK))
+
+        score = [ps.tile([P, 2, S], F32, name=f"score{t}") for t in range(PACK)]
+        b_rows = [sb.tile([P, S], F32, name=f"b_rows{t}") for t in range(PACK)]
+        a_rows = [sb.tile([P, S], F32, name=f"a_rows{t}") for t in range(PACK)]
+        for t in range(PACK):
+            rows = slice(P * t, P * (t + 1))
+            nc.tensor.matmul_mx(score[t][:, 0, :], lhsT=keys[:, rows].bitcast(FP8X4), lhsT_scale=scales[:, rows], rhs=x_two[:].bitcast(FP8X4), rhs_scale=scales[:, H : H + S], start=True, stop=True)
+            nc.vector.tensor_copy(b_rows[t][:], score[t][:, 0, :])
+        for t in range(PACK):
+            rows = slice(P * t, P * (t + 1))
+            nc.tensor.matmul_mx(score[t][:, 1, :], lhsT=keys[:, rows].bitcast(FP8X4), lhsT_scale=scales[:, rows], rhs=x_idx[:].bitcast(FP8X4), rhs_scale=scales[:, H + S : H + 2 * S], start=True, stop=True)
+            nc.vector.tensor_scalar(a_rows[t][:], score[t][:, 1, :], factor[:, t : t + 1], None, ALU.mult)
+
+        b_far = sb.tile([P, PACK, S], F32, name="b_far")
+        b_sum = sb.tile([P, PACK, S], F32, name="b_sum")
+        for u in range(2):
+            cols = slice(HALF * u, HALF * (u + 1))
+            for t in range(PACK):
+                nc.scalar.activation(b_far[:, t, cols], b_rows[t][:].indirect(n2_list[:, 8 * u : 8 * (u + 1)]), ACT.Copy)
+                nc.gpsimd.tensor_tensor(b_sum[:, t, cols], b_far[:, t, cols], b_rows[t][:, cols], ALU.add)
+
+        a_first = sb.tile([P, PACK, HALF], F32, name="a_first")
+        a_sum = sb.tile([P, PACK, S], F32, name="a_sum")
+        gate = sb.tile([P, PACK, S], F32, name="gate")
+        hidden = [ps.tile([P, S], F32, name=f"hidden{t}") for t in range(PACK)]
+        h_rows = [sb.tile([P, S], F32, name=f"h_rows{t}") for t in range(PACK)]
+
+        def fetch_a(u, far):
+            cols = slice(HALF * u, HALF * (u + 1))
+            for t in range(PACK):
+                nc.scalar.activation(far[:, t, 0:HALF], a_rows[t][:].indirect(n1_list[:, 8 * u : 8 * (u + 1)]), ACT.Copy)
+                nc.vector.scalar_tensor_tensor(a_sum[:, t, cols], score[t][:, 1, cols], factor[:, t : t + 1], far[:, t, 0:HALF], ALU.mult, ALU.add)
+
+        def layer(lo, hi):
+            width = hi - lo
+            z = sb.tile([P, width, PACK], BF16, name=f"z{lo}", align_bytes=64)
+            nc.vector.tensor_tensor(
+                z[:].rearrange("p (c i) t -> p c t i", i=4),
+                a_sum[:, :, lo:hi].rearrange("p t (c i) -> p c t i", i=4),
+                gate[:, :, lo:hi].rearrange("p t (c i) -> p c t i", i=4),
+                ALU.mult,
+            )
+            z_words = sb.tile([P, width], U32, name=f"z_words{lo}", align_bytes=64)
+            z_scales = sb.tile([P, width], U8, name=f"z_scales{lo}", align_bytes=64)
+            nc.vector.quantize_mx(z_words[:].bitcast(FP8X4), z_scales[:], z[:].rearrange("p c t -> p (c t)"))
+            for t in range(PACK):
+                rows = slice(P * t, P * (t + 1))
+                nc.tensor.matmul_mx(hidden[t][:, lo:hi], lhsT=w_dealt[:, rows].bitcast(FP8X4), lhsT_scale=w_scales[:, rows], rhs=z_words[:].bitcast(FP8X4), rhs_scale=z_scales[:], start=True, stop=True)
+
+        fetch_a(0, a_first)
+        lo, hi = PIECES[0]
+        nc.scalar.activation(gate[:, :, lo:hi], b_sum[:, :, lo:hi], ACT.Sigmoid, scale=0.0625)
+        layer(lo, hi)
+        fetch_a(1, b_sum)
+        for lo, hi in PIECES[1:]:
+            nc.scalar.activation(gate[:, :, lo:hi], b_sum[:, :, lo:hi], ACT.Sigmoid, scale=0.0625)
+            layer(lo, hi)
+        for t in range(PACK):
+            nc.vector.tensor_copy(h_rows[t][:], hidden[t][:])
+
+        y_rounded = sb.tile([P, S, PACK], BF16, name="y_rounded", align_bytes=64)
+        out_rows = out_0.rearrange("(p t) j -> p t j", t=PACK)
+        y_words = sb.tile([P, S], U32, name="y_words", align_bytes=64)
+        y_scales = sb.tile([P, S], U8, name="y_scales", align_bytes=64)
+        for t in range(PACK):
+            pair = sb.tile([P, 2, W], F32, name=f"pair{t}")
+            nc.scalar.activation(pair[:, 0, :], h_rows[t][:].indirect(n3_list[:]), ACT.Copy)
+            nc.scalar.activation(pair[:, 1, :], h_rows[t][:].indirect(n4_list[:]), ACT.Copy)
+            mixed = sb.tile([P, 2, W], F32, name=f"mixed{t}")
+            nc.vector.tensor_tensor(mixed[:, 0, :], pair[:, 0, :], pair[:, 1, :], ALU.add)
+            nc.vector.tensor_tensor(mixed[:, 1, :], pair[:, 0, :], pair[:, 1, :], ALU.subtract)
+            y = sb.tile([P, S], F32, name=f"y{t}")
+            nc.scalar.activation(y[:].indirect(n3_list[:]), mixed[:, 0, :], ACT.Copy, scale=0.75)
+            nc.scalar.activation(y[:].indirect(n4_list[:]), mixed[:, 1, :], ACT.Copy)
+            nc.sync.dma_start(out_rows[:, t, :], y[:])
+            for u in range(2):
+                nc.vector.tensor_copy(y_rounded[:, HALF * u : HALF * (u + 1), t], y[:, HALF * u : HALF * (u + 1)])
+
+        for u in range(2):
+            cols = slice(HALF * u, HALF * (u + 1))
+            nc.vector.quantize_mx(y_words[:, cols].bitcast(FP8X4), y_scales[:, cols], y_rounded[:, cols, :].rearrange("p c t -> p (c t)"))
+        nc.sync.dma_start(words_of(out_1), y_words[:].bitcast(I32))
+        for q in range(4):
+            queue = nc.scalar if q % 2 == 0 else nc.sync
+            queue.dma_start(out_2[0, 4 * q : 4 * q + 4, :].bitcast(I32), y_scales[:].bitcast(I32)[32 * q : 32 * q + 4, :])

@@ -37,27 +37,27 @@ def tile_picked_twkstriebhaar_none_po_kernel(tc, x_words, x_scales, d_words, d_s
 
         d_bytes = sb.tile([P, G], U8, name="d_bytes", align_bytes=64)
         x_bytes = sb.tile([P, T], U8, name="x_bytes", align_bytes=64)
-        nc.gpsimd.memset(d_bytes[:].bitcast(I32), 0)
-        nc.vector.memset(x_bytes[:].bitcast(I32), 0)
+        nc.vector.memset(d_bytes[:].bitcast(I32), 0)
+        nc.gpsimd.memset(x_bytes[:].bitcast(I32), 0)
         nc.scalar.dma_start(x_bytes[:].bitcast(I32)[0:P:8, :], x_scales[0].bitcast(I32))
 
         k1_list = load_list("k1_list", k1)
         nc.sync.dma_start(d_bytes[:].bitcast(I32)[0:P:8, :], d_scales[0].bitcast(I32))
         two_list = load_list("two_list", two)
         offs_list = load_list("offs_list", offs)
+        n2_list = load_list("n2_list", n2)
+        n1_list = load_list("n1_list", n1)
         d_table = sb.tile([P, G], U32, name="d_table", align_bytes=64)
         x_table = sb.tile([P, T], U32, name="x_table", align_bytes=64)
         nc.sync.dma_start(d_table[:].bitcast(I32), words_of(d_words))
         nc.sync.dma_start(x_table[:].bitcast(I32), words_of(x_words))
-        n2_list = load_list("n2_list", n2)
-        n1_list = load_list("n1_list", n1)
         n3_list = load_list("n3_list", n3)
         n4_list = load_list("n4_list", n4)
+        w_table = sb.tile([P, N], U32, name="w_table", align_bytes=64)
+        nc.sync.dma_start(w_table[:].bitcast(I32), words_of(w1_words))
 
         gain = sb.tile([P, PACK], F32, name="gain")
         nc.gpsimd.dma_start(gain[:], gn.rearrange("(p t) o -> p (t o)", t=PACK))
-        w_table = sb.tile([P, N], U32, name="w_table", align_bytes=64)
-        nc.gpsimd.dma_start(w_table[:].bitcast(I32), words_of(w1_words))
         w_bytes = sb.tile([P, N], U8, name="w_bytes", align_bytes=64)
         nc.gpsimd.memset(w_bytes[:].bitcast(I32), 0)
         for q in range(4):
@@ -68,11 +68,11 @@ def tile_picked_twkstriebhaar_none_po_kernel(tc, x_words, x_scales, d_words, d_s
         d_picked_bytes = sb.tile([P, H], U8, name="d_picked_bytes", align_bytes=64)
         x_picked_bytes = sb.tile([P, 2 * S], U8, name="x_picked_bytes", align_bytes=64)
         nc.vector.tensor_copy(d_picked_bytes[:], d_bytes[:].indirect(k1_list[:]))
-        nc.vector.tensor_copy(x_picked_bytes[:, 0:S], x_bytes[:].indirect(two_list[:]))
-        nc.vector.tensor_copy(x_picked_bytes[:, S : 2 * S], x_bytes[:].indirect(offs_list[:]))
         spread = sb.tile([P, H + 2 * S], U8, name="spread", align_bytes=64)
         scales = sb.tile([P, H + 2 * S], U8, name="scales", align_bytes=64)
         nc.vector.tensor_copy(spread[:, 0:H].rearrange("p (t m) -> p t m", t=PACK), d_picked_bytes[:].rearrange("p (m t) -> p t m", t=PACK))
+        nc.vector.tensor_copy(x_picked_bytes[:, 0:S], x_bytes[:].indirect(two_list[:]))
+        nc.vector.tensor_copy(x_picked_bytes[:, S : 2 * S], x_bytes[:].indirect(offs_list[:]))
         nc.vector.tensor_copy(spread[:, H : H + 2 * S].bitcast(I32), x_picked_bytes[:].bitcast(I32))
         for q in range(4):
             nc.scalar.dma_start(scales[:].bitcast(I32)[32 * q : 32 * q + 4, :], spread[:].bitcast(I32)[32 * q : 32 * q + 32 : 8, :])
@@ -87,49 +87,55 @@ def tile_picked_twkstriebhaar_none_po_kernel(tc, x_words, x_scales, d_words, d_s
         nc.vector.tensor_copy(x_idx[:], x_table[:].indirect(offs_list[:]))
 
         w_dealt = sb.tile([P, N], U32, name="w_dealt", align_bytes=64)
-        nc.scalar.copy(w_dealt[:].rearrange("p (t m i) -> p m t i", t=PACK, i=4), w_table[:].rearrange("p (m i t) -> p m t i", t=PACK, i=4))
+        nc.gpsimd.tensor_copy(w_dealt[:].rearrange("p (t m i) -> p m t i", t=PACK, i=4), w_table[:].rearrange("p (m i t) -> p m t i", t=PACK, i=4))
         w_scales = sb.tile([P, N], U8, name="w_scales", align_bytes=64)
         nc.gpsimd.tensor_copy(w_scales[:].rearrange("p (t m) -> p t m", t=PACK), w_bytes[:].rearrange("p (m t) -> p t m", t=PACK))
 
-        score = [ps.tile([P, 2, S], F32, name=f"score{t}") for t in range(PACK)]
+        b_bank = [ps.tile([P, S], F32, name=f"b_bank{t}", tag=f"shared{t}") for t in range(PACK)]
+        a_bank = [ps.tile([P, S], F32, name=f"a_bank{t}") for t in range(PACK)]
         b_rows = [sb.tile([P, S], F32, name=f"b_rows{t}") for t in range(PACK)]
         a_rows = [sb.tile([P, S], F32, name=f"a_rows{t}") for t in range(PACK)]
         for t in range(PACK):
             rows = slice(P * t, P * (t + 1))
-            nc.tensor.matmul_mx(score[t][:, 0, :], lhsT=keys[:, rows].bitcast(FP8X4), lhsT_scale=scales[:, rows], rhs=x_two[:].bitcast(FP8X4), rhs_scale=scales[:, H : H + S], start=True, stop=True)
-            nc.vector.tensor_copy(b_rows[t][:], score[t][:, 0, :])
+            nc.tensor.matmul_mx(b_bank[t][:], lhsT=keys[:, rows].bitcast(FP8X4), lhsT_scale=scales[:, rows], rhs=x_two[:].bitcast(FP8X4), rhs_scale=scales[:, H : H + S], start=True, stop=True)
+            if t == 0:
+                nc.scalar.copy(b_rows[t][:], b_bank[t][:])
+            else:
+                nc.vector.tensor_copy(b_rows[t][:], b_bank[t][:])
         for t in range(PACK):
             rows = slice(P * t, P * (t + 1))
-            nc.tensor.matmul_mx(score[t][:, 1, :], lhsT=keys[:, rows].bitcast(FP8X4), lhsT_scale=scales[:, rows], rhs=x_idx[:].bitcast(FP8X4), rhs_scale=scales[:, H + S : H + 2 * S], start=True, stop=True)
-            nc.vector.tensor_scalar(a_rows[t][:], score[t][:, 1, :], factor[:, t : t + 1], None, ALU.mult)
+            nc.tensor.matmul_mx(a_bank[t][:], lhsT=keys[:, rows].bitcast(FP8X4), lhsT_scale=scales[:, rows], rhs=x_idx[:].bitcast(FP8X4), rhs_scale=scales[:, H + S : H + 2 * S], start=True, stop=True)
+            nc.vector.tensor_scalar(a_rows[t][:], a_bank[t][:], factor[:, t : t + 1], None, ALU.mult)
 
         b_far = sb.tile([P, PACK, S], F32, name="b_far")
-        b_sum = sb.tile([P, PACK, S], F32, name="b_sum")
-        for u in range(2):
-            cols = slice(HALF * u, HALF * (u + 1))
-            for t in range(PACK):
-                nc.scalar.activation(b_far[:, t, cols], b_rows[t][:].indirect(n2_list[:, 8 * u : 8 * (u + 1)]), ACT.Copy)
-                nc.gpsimd.tensor_tensor(b_sum[:, t, cols], b_far[:, t, cols], b_rows[t][:, cols], ALU.add)
+        b_sum = sb.tile([P, 2, PACK, HALF], F32, name="b_sum")
+        for t in range(PACK):
+            for u in range(2):
+                nc.scalar.activation(b_far[:, t, HALF * u : HALF * (u + 1)], b_rows[t][:].indirect(n2_list[:, 8 * u : 8 * (u + 1)]), ACT.Copy)
+            nc.vector.tensor_tensor(b_sum[:, :, t, :], b_far[:, t, :].rearrange("p (u c) -> p u c", u=2), b_rows[t][:].rearrange("p (u c) -> p u c", u=2), ALU.add)
 
         a_first = sb.tile([P, PACK, HALF], F32, name="a_first")
-        a_sum = sb.tile([P, PACK, S], F32, name="a_sum")
-        gate = sb.tile([P, PACK, S], F32, name="gate")
-        hidden = [ps.tile([P, S], F32, name=f"hidden{t}") for t in range(PACK)]
+        a_sum = [sb.tile([P, PACK, HALF], F32, name=f"a_sum{u}") for u in range(2)]
+        hidden = [ps.tile([P, S], F32, name=f"hidden{t}", tag=f"shared{t}") for t in range(PACK)]
         h_rows = [sb.tile([P, S], F32, name=f"h_rows{t}") for t in range(PACK)]
 
         def fetch_a(u, far):
             cols = slice(HALF * u, HALF * (u + 1))
             for t in range(PACK):
-                nc.scalar.activation(far[:, t, 0:HALF], a_rows[t][:].indirect(n1_list[:, 8 * u : 8 * (u + 1)]), ACT.Copy)
-                nc.vector.scalar_tensor_tensor(a_sum[:, t, cols], score[t][:, 1, cols], factor[:, t : t + 1], far[:, t, 0:HALF], ALU.mult, ALU.add)
+                nc.scalar.activation(far[:, t, :], a_rows[t][:].indirect(n1_list[:, 8 * u : 8 * (u + 1)]), ACT.Copy)
+                nc.vector.scalar_tensor_tensor(a_sum[u][:, t, :], a_bank[t][:, cols], factor[:, t : t + 1], far[:, t, :], ALU.mult, ALU.add)
 
         def layer(lo, hi):
             width = hi - lo
+            u = lo // HALF
+            inside = slice(lo - HALF * u, hi - HALF * u)
+            gate = sb.tile([P, PACK, width], F32, name=f"gate{lo}")
+            nc.scalar.activation(gate[:], b_sum[:, u, :, inside], ACT.Sigmoid, scale=0.0625)
             z = sb.tile([P, width, PACK], BF16, name=f"z{lo}", align_bytes=64)
             nc.vector.tensor_tensor(
                 z[:].rearrange("p (c i) t -> p c t i", i=4),
-                a_sum[:, :, lo:hi].rearrange("p t (c i) -> p c t i", i=4),
-                gate[:, :, lo:hi].rearrange("p t (c i) -> p c t i", i=4),
+                a_sum[u][:, :, inside].rearrange("p t (c i) -> p c t i", i=4),
+                gate[:].rearrange("p t (c i) -> p c t i", i=4),
                 ALU.mult,
             )
             z_words = sb.tile([P, width], U32, name=f"z_words{lo}", align_bytes=64)
@@ -139,13 +145,10 @@ def tile_picked_twkstriebhaar_none_po_kernel(tc, x_words, x_scales, d_words, d_s
                 rows = slice(P * t, P * (t + 1))
                 nc.tensor.matmul_mx(hidden[t][:, lo:hi], lhsT=w_dealt[:, rows].bitcast(FP8X4), lhsT_scale=w_scales[:, rows], rhs=z_words[:].bitcast(FP8X4), rhs_scale=z_scales[:], start=True, stop=True)
 
-        fetch_a(0, a_first)
-        lo, hi = PIECES[0]
-        nc.scalar.activation(gate[:, :, lo:hi], b_sum[:, :, lo:hi], ACT.Sigmoid, scale=0.0625)
-        layer(lo, hi)
-        fetch_a(1, b_sum)
+        fetch_a(0, a_first[:])
+        layer(*PIECES[0])
+        fetch_a(1, b_sum[:, 0, :, :])
         for lo, hi in PIECES[1:]:
-            nc.scalar.activation(gate[:, :, lo:hi], b_sum[:, :, lo:hi], ACT.Sigmoid, scale=0.0625)
             layer(lo, hi)
         for t in range(PACK):
             nc.vector.tensor_copy(h_rows[t][:], hidden[t][:])

@@ -65,6 +65,9 @@ def tile_picked_twkstriebhaar_none_po_kernel(tc, x_words, x_scales, d_words, d_s
         factor = sb.tile([P, PACK], F32, name="factor")
         nc.gpsimd.tensor_scalar(factor[:], gain[:], 0.0625, 0.0, ALU.mult, ALU.add)
 
+        warm = sb.tile([P, 1], F32, name="warm")
+        nc.scalar.activation(warm[:], gain[:, 0:1], ACT.Sigmoid)
+
         d_picked_bytes = sb.tile([P, H], U8, name="d_picked_bytes", align_bytes=64)
         x_picked_bytes = sb.tile([P, 2 * S], U8, name="x_picked_bytes", align_bytes=64)
         nc.vector.tensor_copy(d_picked_bytes[:], d_bytes[:].indirect(k1_list[:]))

@@ -38,8 +38,10 @@ def tile_picked_twkstriebhaar_none_po_kernel(tc, x_words, x_scales, d_words, d_s
         d_bytes = sb.tile([P, G], U8, name="d_bytes", align_bytes=64)
         x_bytes = sb.tile([P, T], U8, name="x_bytes", align_bytes=64)
         nc.vector.memset(d_bytes[:].bitcast(I32), 0)
-        nc.gpsimd.memset(x_bytes[:].bitcast(I32), 0)
-        nc.scalar.dma_start(x_bytes[:].bitcast(I32)[0:P:8, :], x_scales[0].bitcast(I32))
+        nc.vector.memset(x_bytes[:].bitcast(I32), 0)
+        b_rows = [sb.tile([P, 2 * S], F32, name=f"b_rows{t}") for t in range(PACK)]
+        for t in range(PACK):
+            nc.vector.memset(b_rows[t][:, S : 2 * S], 0.0)
 
         k1_list = load_list("k1_list", k1)
         nc.sync.dma_start(d_bytes[:].bitcast(I32)[0:P:8, :], d_scales[0].bitcast(I32))
@@ -47,8 +49,9 @@ def tile_picked_twkstriebhaar_none_po_kernel(tc, x_words, x_scales, d_words, d_s
         offs_list = load_list("offs_list", offs)
         n2_list = load_list("n2_list", n2)
         n1_list = load_list("n1_list", n1)
+        nc.sync.dma_start(x_bytes[:].bitcast(I32)[0:P:8, :], x_scales[0].bitcast(I32))
         d_table = sb.tile([P, G], U32, name="d_table", align_bytes=64)
-        x_table = sb.tile([P, T], U32, name="x_table", align_bytes=64)
+        x_table = sb.tile([P, T], U32, name="x_table", tag="x_table", align_bytes=64)
         nc.sync.dma_start(d_table[:].bitcast(I32), words_of(d_words))
         nc.sync.dma_start(x_table[:].bitcast(I32), words_of(x_words))
         n3_list = load_list("n3_list", n3)
@@ -70,52 +73,56 @@ def tile_picked_twkstriebhaar_none_po_kernel(tc, x_words, x_scales, d_words, d_s
 
         d_picked_bytes = sb.tile([P, H], U8, name="d_picked_bytes", align_bytes=64)
         x_picked_bytes = sb.tile([P, 2 * S], U8, name="x_picked_bytes", align_bytes=64)
-        nc.vector.tensor_copy(d_picked_bytes[:], d_bytes[:].indirect(k1_list[:]))
+        for u in range(2):
+            nc.vector.tensor_copy(d_picked_bytes[:, 256 * u : 256 * (u + 1)], d_bytes[:].indirect(k1_list[:, 16 * u : 16 * (u + 1)]))
         spread = sb.tile([P, H + 2 * S], U8, name="spread", align_bytes=64)
         scales = sb.tile([P, H + 2 * S], U8, name="scales", align_bytes=64)
-        nc.vector.tensor_copy(spread[:, 0:H].rearrange("p (t m) -> p t m", t=PACK), d_picked_bytes[:].rearrange("p (m t) -> p t m", t=PACK))
+        for u in range(2):
+            nc.vector.tensor_copy(spread[:, 0:H].rearrange("p (t m) -> p t m", t=PACK)[:, :, 64 * u : 64 * (u + 1)], d_picked_bytes[:, 256 * u : 256 * (u + 1)].rearrange("p (m t) -> p t m", t=PACK))
         nc.vector.tensor_copy(x_picked_bytes[:, 0:S], x_bytes[:].indirect(two_list[:]))
         nc.vector.tensor_copy(x_picked_bytes[:, S : 2 * S], x_bytes[:].indirect(offs_list[:]))
-        nc.vector.tensor_copy(spread[:, H : H + 2 * S].bitcast(I32), x_picked_bytes[:].bitcast(I32))
+        for u in range(2):
+            nc.vector.tensor_copy(spread[:, H + S * u : H + S * (u + 1)].bitcast(I32), x_picked_bytes[:, S * u : S * (u + 1)].bitcast(I32))
         for q in range(4):
             nc.scalar.dma_start(scales[:].bitcast(I32)[32 * q : 32 * q + 4, :], spread[:].bitcast(I32)[32 * q : 32 * q + 32 : 8, :])
 
         d_picked = sb.tile([P, H], U32, name="d_picked", align_bytes=64)
-        nc.vector.tensor_copy(d_picked[:], d_table[:].indirect(k1_list[:]))
+        for u in range(2):
+            nc.vector.tensor_copy(d_picked[:, 256 * u : 256 * (u + 1)], d_table[:].indirect(k1_list[:, 16 * u : 16 * (u + 1)]))
         keys = sb.tile([P, H], U32, name="keys", align_bytes=64)
-        nc.vector.tensor_copy(keys[:].rearrange("p (t m i) -> p m t i", t=PACK, i=4), d_picked[:].rearrange("p (m i t) -> p m t i", t=PACK, i=4))
+        for u in range(2):
+            nc.vector.tensor_copy(keys[:].rearrange("p (t m i) -> p m t i", t=PACK, i=4)[:, 16 * u : 16 * (u + 1), :, :], d_picked[:, 256 * u : 256 * (u + 1)].rearrange("p (m i t) -> p m t i", t=PACK, i=4))
         x_two = sb.tile([P, S], U32, name="x_two", align_bytes=64)
         nc.vector.tensor_copy(x_two[:], x_table[:].indirect(two_list[:]))
-        x_idx = sb.tile([P, S], U32, name="x_idx", align_bytes=64)
+        x_idx = sb.tile([P, S], U32, name="x_idx", tag="x_idx", align_bytes=64)
         nc.vector.tensor_copy(x_idx[:], x_table[:].indirect(offs_list[:]))
 
-        w_dealt = sb.tile([P, N], U32, name="w_dealt", align_bytes=64)
-        nc.gpsimd.tensor_copy(w_dealt[:].rearrange("p (t m i) -> p m t i", t=PACK, i=4), w_table[:].rearrange("p (m i t) -> p m t i", t=PACK, i=4))
-        w_scales = sb.tile([P, N], U8, name="w_scales", align_bytes=64)
+        w_scales = sb.tile([P, N], U8, name="w_scales", tag="x_table", align_bytes=64)
         nc.gpsimd.tensor_copy(w_scales[:].rearrange("p (t m) -> p t m", t=PACK), w_bytes[:].rearrange("p (m t) -> p t m", t=PACK))
 
         b_bank = [ps.tile([P, S], F32, name=f"b_bank{t}", tag=f"shared{t}") for t in range(PACK)]
         a_bank = [ps.tile([P, S], F32, name=f"a_bank{t}") for t in range(PACK)]
-        b_rows = [sb.tile([P, S], F32, name=f"b_rows{t}") for t in range(PACK)]
         a_rows = [sb.tile([P, S], F32, name=f"a_rows{t}") for t in range(PACK)]
         for t in range(PACK):
             rows = slice(P * t, P * (t + 1))
             nc.tensor.matmul_mx(b_bank[t][:], lhsT=keys[:, rows].bitcast(FP8X4), lhsT_scale=scales[:, rows], rhs=x_two[:].bitcast(FP8X4), rhs_scale=scales[:, H : H + S], start=True, stop=True)
             if t == 0:
-                nc.scalar.copy(b_rows[t][:], b_bank[t][:])
+                nc.scalar.copy(b_rows[t][:, 0:S], b_bank[t][:])
             else:
-                nc.vector.tensor_copy(b_rows[t][:], b_bank[t][:])
+                nc.vector.tensor_copy(b_rows[t][:, 0:S], b_bank[t][:])
         for t in range(PACK):
             rows = slice(P * t, P * (t + 1))
             nc.tensor.matmul_mx(a_bank[t][:], lhsT=keys[:, rows].bitcast(FP8X4), lhsT_scale=scales[:, rows], rhs=x_idx[:].bitcast(FP8X4), rhs_scale=scales[:, H + S : H + 2 * S], start=True, stop=True)
             nc.vector.tensor_scalar(a_rows[t][:], a_bank[t][:], factor[:, t : t + 1], None, ALU.mult)
 
+        w_dealt = sb.tile([P, N], U32, name="w_dealt", tag="x_idx", align_bytes=64)
+        nc.gpsimd.tensor_copy(w_dealt[:].rearrange("p (t m i) -> p m t i", t=PACK, i=4), w_table[:].rearrange("p (m i t) -> p m t i", t=PACK, i=4))
+
         b_far = sb.tile([P, PACK, S], F32, name="b_far")
         b_sum = sb.tile([P, 2, PACK, HALF], F32, name="b_sum")
         for t in range(PACK):
-            for u in range(2):
-                nc.scalar.activation(b_far[:, t, HALF * u : HALF * (u + 1)], b_rows[t][:].indirect(n2_list[:, 8 * u : 8 * (u + 1)]), ACT.Copy)
-            nc.vector.tensor_tensor(b_sum[:, :, t, :], b_far[:, t, :].rearrange("p (u c) -> p u c", u=2), b_rows[t][:].rearrange("p (u c) -> p u c", u=2), ALU.add)
+            nc.scalar.activation(b_far[:, t, :], b_rows[t][:].indirect(n2_list[:]), ACT.Copy)
+            nc.vector.tensor_tensor(b_sum[:, :, t, :], b_far[:, t, :].rearrange("p (u c) -> p u c", u=2), b_bank[t][:].rearrange("p (u c) -> p u c", u=2), ALU.add)
 
         a_first = sb.tile([P, PACK, HALF], F32, name="a_first")
         a_sum = [sb.tile([P, PACK, HALF], F32, name=f"a_sum{u}") for u in range(2)]
@@ -144,17 +151,24 @@ def tile_picked_twkstriebhaar_none_po_kernel(tc, x_words, x_scales, d_words, d_s
             z_words = sb.tile([P, width], U32, name=f"z_words{lo}", align_bytes=64)
             z_scales = sb.tile([P, width], U8, name=f"z_scales{lo}", align_bytes=64)
             nc.vector.quantize_mx(z_words[:].bitcast(FP8X4), z_scales[:], z[:].rearrange("p c t -> p (c t)"))
-            for t in range(PACK):
-                rows = slice(P * t, P * (t + 1))
-                nc.tensor.matmul_mx(hidden[t][:, lo:hi], lhsT=w_dealt[:, rows].bitcast(FP8X4), lhsT_scale=w_scales[:, rows], rhs=z_words[:].bitcast(FP8X4), rhs_scale=z_scales[:], start=True, stop=True)
+            return lo, hi, z_words, z_scales
+
+        def multiply(t, lo, hi, z_words, z_scales):
+            rows = slice(P * t, P * (t + 1))
+            nc.tensor.matmul_mx(hidden[t][:, lo:hi], lhsT=w_dealt[:, rows].bitcast(FP8X4), lhsT_scale=w_scales[:, rows], rhs=z_words[:].bitcast(FP8X4), rhs_scale=z_scales[:], start=True, stop=True)
 
         fetch_a(0, a_first[:])
-        layer(*PIECES[0])
-        fetch_a(1, b_sum[:, 0, :, :])
-        for lo, hi in PIECES[1:]:
-            layer(lo, hi)
+        first = layer(*PIECES[0])
         for t in range(PACK):
-            nc.vector.tensor_copy(h_rows[t][:], hidden[t][:])
+            multiply(t, *first)
+        fetch_a(1, b_sum[:, 0, :, :])
+        later = [layer(lo, hi) for lo, hi in PIECES[1:]]
+        nc.scalar.copy(h_rows[0][:, 0:HALF], hidden[0][:, 0:HALF])
+        for t in range(PACK):
+            for piece in later:
+                multiply(t, *piece)
+            start = HALF if t == 0 else 0
+            nc.vector.tensor_copy(h_rows[t][:, start:S], hidden[t][:, start:S])
 
         y_rounded = sb.tile([P, S, PACK], BF16, name="y_rounded", align_bytes=64)
         out_rows = out_0.rearrange("(p t) j -> p t j", t=PACK)

@@ -39,6 +39,8 @@ def tile_picked_twkstriebhaar_none_po_kernel(tc, x_words, x_scales, d_words, d_s
         x_bytes = sb.tile([P, T], U8, name="x_bytes", align_bytes=64)
         nc.vector.memset(d_bytes[:].bitcast(I32), 0)
         nc.vector.memset(x_bytes[:].bitcast(I32), 0)
+        w_bytes = sb.tile([P, N], U8, name="w_bytes", align_bytes=64)
+        nc.vector.memset(w_bytes[:].bitcast(I32), 0)
         b_rows = [sb.tile([P, 2 * S], F32, name=f"b_rows{t}") for t in range(PACK)]
         for t in range(PACK):
             nc.vector.memset(b_rows[t][:, S : 2 * S], 0.0)
@@ -61,8 +63,6 @@ def tile_picked_twkstriebhaar_none_po_kernel(tc, x_words, x_scales, d_words, d_s
 
         gain = sb.tile([P, PACK], F32, name="gain")
         nc.gpsimd.dma_start(gain[:], gn.rearrange("(p t) o -> p (t o)", t=PACK))
-        w_bytes = sb.tile([P, N], U8, name="w_bytes", align_bytes=64)
-        nc.gpsimd.memset(w_bytes[:].bitcast(I32), 0)
         for q in range(4):
             nc.gpsimd.dma_start(w_bytes[:].bitcast(I32)[32 * q : 32 * q + 4, :], w1_scales[0, 4 * q : 4 * q + 4, :].bitcast(I32))
         factor = sb.tile([P, PACK], F32, name="factor")
@@ -191,7 +191,7 @@ def tile_picked_twkstriebhaar_none_po_kernel(tc, x_words, x_scales, d_words, d_s
         for u in range(2):
             cols = slice(HALF * u, HALF * (u + 1))
             nc.vector.quantize_mx(y_words[:, cols].bitcast(FP8X4), y_scales[:, cols], y_rounded[:, cols, :].rearrange("p c t -> p (c t)"))
-        nc.sync.dma_start(words_of(out_1), y_words[:].bitcast(I32))
+            nc.sync.dma_start(words_of(out_1)[:, cols], y_words[:, cols].bitcast(I32))
         for q in range(4):
-            queue = nc.scalar if q % 2 == 0 else nc.sync
+            queue = nc.sync if q == 3 else nc.scalar
             queue.dma_start(out_2[0, 4 * q : 4 * q + 4, :].bitcast(I32), y_scales[:].bitcast(I32)[32 * q : 32 * q + 4, :])

from contextlib import ExitStack

import concourse.mybir as mybir

K, T, S, N, G, H, W = 512, 2048, 256, 512, 2048, 512, 128
FLOPS = 2 * K * H * S * 2 + 2 * H * N * S

F32 = mybir.dt.float32
BF16 = mybir.dt.bfloat16
I32 = mybir.dt.int32
U32 = mybir.dt.uint32
U16 = mybir.dt.uint16
U8 = mybir.dt.uint8
FP8X4 = mybir.dt.float8_e4m3fn_x4
ACT = mybir.ActivationFunctionType
ALU = mybir.AluOpType

P = 128
PACK = 4
HALF = 128
PIECES = ((0, 128), (128, 192), (192, 256))


def tile_picked_twkstriebhaar_none_po_kernel(tc, x_words, x_scales, d_words, d_scales, gn, w1_words, w1_scales, offs, k1, two, n1, n2, n3, n4, out_0, out_1, out_2):
    nc = tc.nc
    with ExitStack() as ctx:
        sb = ctx.enter_context(tc.tile_pool(name="sb", bufs=1))
        ps = ctx.enter_context(tc.psum_pool(name="ps", bufs=1))

        def words_of(ap):
            return ap[0].rearrange("p n t -> p (n t)").bitcast(I32)

        def load_list(name, ap):
            tile = sb.tile(list(ap.shape), U16, name=name)
            nc.sync.dma_start(tile[:], ap)
            return tile

        d_bytes = sb.tile([P, G], U8, name="d_bytes", align_bytes=64)
        x_bytes = sb.tile([P, T], U8, name="x_bytes", align_bytes=64)
        nc.vector.memset(d_bytes[:].bitcast(I32), 0)
        nc.vector.memset(x_bytes[:].bitcast(I32), 0)
        w_bytes = sb.tile([P, N], U8, name="w_bytes", align_bytes=64)
        nc.vector.memset(w_bytes[:].bitcast(I32), 0)
        b_rows = [sb.tile([P, 2 * S], F32, name=f"b_rows{t}") for t in range(PACK)]
        for t in range(PACK):
            nc.vector.memset(b_rows[t][:, S : 2 * S], 0.0)

        k1_list = load_list("k1_list", k1)
        nc.sync.dma_start(d_bytes[:].bitcast(I32)[0:P:8, :], d_scales[0].bitcast(I32))
        two_list = load_list("two_list", two)
        offs_list = load_list("offs_list", offs)
        n2_list = load_list("n2_list", n2)
        n1_list = load_list("n1_list", n1)
        nc.sync.dma_start(x_bytes[:].bitcast(I32)[0:P:8, :], x_scales[0].bitcast(I32))
        d_table = sb.tile([P, G], U32, name="d_table", align_bytes=64)
        x_table = sb.tile([P, T], U32, name="x_table", tag="x_table", align_bytes=64)
        nc.sync.dma_start(d_table[:].bitcast(I32), words_of(d_words))
        nc.sync.dma_start(x_table[:].bitcast(I32), words_of(x_words))
        n3_list = load_list("n3_list", n3)
        n4_list = load_list("n4_list", n4)
        w_table = sb.tile([P, N], U32, name="w_table", align_bytes=64)
        nc.sync.dma_start(w_table[:].bitcast(I32), words_of(w1_words))

        gain = sb.tile([P, PACK], F32, name="gain")
        nc.gpsimd.dma_start(gain[:], gn.rearrange("(p t) o -> p (t o)", t=PACK))
        for q in range(4):
            nc.gpsimd.dma_start(w_bytes[:].bitcast(I32)[32 * q : 32 * q + 4, :], w1_scales[0, 4 * q : 4 * q + 4, :].bitcast(I32))
        factor = sb.tile([P, PACK], F32, name="factor")
        nc.gpsimd.tensor_scalar(factor[:], gain[:], 0.0625, 0.0, ALU.mult, ALU.add)

        warm = sb.tile([P, 1], F32, name="warm")
        nc.scalar.activation(warm[:], gain[:, 0:1], ACT.Sigmoid)

        d_picked_bytes = sb.tile([P, H], U8, name="d_picked_bytes", align_bytes=64)
        x_picked_bytes = sb.tile([P, 2 * S], U8, name="x_picked_bytes", align_bytes=64)
        for u in range(2):
            nc.vector.tensor_copy(d_picked_bytes[:, 256 * u : 256 * (u + 1)], d_bytes[:].indirect(k1_list[:, 16 * u : 16 * (u + 1)]))
        spread = sb.tile([P, H + 2 * S], U8, name="spread", align_bytes=64)
        scales = sb.tile([P, H + 2 * S], U8, name="scales", align_bytes=64)
        for u in range(2):
            nc.vector.tensor_copy(spread[:, 0:H].rearrange("p (t m) -> p t m", t=PACK)[:, :, 64 * u : 64 * (u + 1)], d_picked_bytes[:, 256 * u : 256 * (u + 1)].rearrange("p (m t) -> p t m", t=PACK))
        nc.vector.tensor_copy(x_picked_bytes[:, 0:S], x_bytes[:].indirect(two_list[:]))
        nc.vector.tensor_copy(x_picked_bytes[:, S : 2 * S], x_bytes[:].indirect(offs_list[:]))
        for u in range(2):
            nc.vector.tensor_copy(spread[:, H + S * u : H + S * (u + 1)].bitcast(I32), x_picked_bytes[:, S * u : S * (u + 1)].bitcast(I32))
        for q in range(4):
            nc.scalar.dma_start(scales[:].bitcast(I32)[32 * q : 32 * q + 4, :], spread[:].bitcast(I32)[32 * q : 32 * q + 32 : 8, :])

        d_picked = sb.tile([P, H], U32, name="d_picked", align_bytes=64)
        for u in range(2):
            nc.vector.tensor_copy(d_picked[:, 256 * u : 256 * (u + 1)], d_table[:].indirect(k1_list[:, 16 * u : 16 * (u + 1)]))
        keys = sb.tile([P, H], U32, name="keys", align_bytes=64)
        for u in range(2):
            nc.vector.tensor_copy(keys[:].rearrange("p (t m i) -> p m t i", t=PACK, i=4)[:, 16 * u : 16 * (u + 1), :, :], d_picked[:, 256 * u : 256 * (u + 1)].rearrange("p (m i t) -> p m t i", t=PACK, i=4))
        x_two = sb.tile([P, S], U32, name="x_two", align_bytes=64)
        nc.vector.tensor_copy(x_two[:], x_table[:].indirect(two_list[:]))
        x_idx = sb.tile([P, S], U32, name="x_idx", tag="x_idx", align_bytes=64)
        nc.vector.tensor_copy(x_idx[:], x_table[:].indirect(offs_list[:]))

        w_scales = sb.tile([P, N], U8, name="w_scales", tag="x_table", align_bytes=64)
        nc.gpsimd.tensor_copy(w_scales[:].rearrange("p (t m) -> p t m", t=PACK), w_bytes[:].rearrange("p (m t) -> p t m", t=PACK))

        b_bank = [ps.tile([P, S], F32, name=f"b_bank{t}", tag=f"shared{t}") for t in range(PACK)]
        a_bank = [ps.tile([P, S], F32, name=f"a_bank{t}") for t in range(PACK)]
        a_rows = [sb.tile([P, S], F32, name=f"a_rows{t}") for t in range(PACK)]
        for t in range(PACK):
            rows = slice(P * t, P * (t + 1))
            nc.tensor.matmul_mx(b_bank[t][:], lhsT=keys[:, rows].bitcast(FP8X4), lhsT_scale=scales[:, rows], rhs=x_two[:].bitcast(FP8X4), rhs_scale=scales[:, H : H + S], start=True, stop=True)
            if t == 0:
                nc.scalar.copy(b_rows[t][:, 0:S], b_bank[t][:])
            else:
                nc.vector.tensor_copy(b_rows[t][:, 0:S], b_bank[t][:])
        for t in range(PACK):
            rows = slice(P * t, P * (t + 1))
            nc.tensor.matmul_mx(a_bank[t][:], lhsT=keys[:, rows].bitcast(FP8X4), lhsT_scale=scales[:, rows], rhs=x_idx[:].bitcast(FP8X4), rhs_scale=scales[:, H + S : H + 2 * S], start=True, stop=True)
            nc.vector.tensor_scalar(a_rows[t][:], a_bank[t][:], factor[:, t : t + 1], None, ALU.mult)

        w_dealt = sb.tile([P, N], U32, name="w_dealt", tag="x_idx", align_bytes=64)
        nc.gpsimd.tensor_copy(w_dealt[:].rearrange("p (t m i) -> p m t i", t=PACK, i=4), w_table[:].rearrange("p (m i t) -> p m t i", t=PACK, i=4))

        b_far = sb.tile([P, PACK, S], F32, name="b_far")
        b_sum = sb.tile([P, 2, PACK, HALF], F32, name="b_sum")
        for t in range(PACK):
            nc.scalar.activation(b_far[:, t, :], b_rows[t][:].indirect(n2_list[:]), ACT.Copy)
            nc.vector.tensor_tensor(b_sum[:, :, t, :], b_far[:, t, :].rearrange("p (u c) -> p u c", u=2), b_bank[t][:].rearrange("p (u c) -> p u c", u=2), ALU.add)

        a_first = sb.tile([P, PACK, HALF], F32, name="a_first")
        a_sum = [sb.tile([P, PACK, HALF], F32, name=f"a_sum{u}") for u in range(2)]
        hidden = [ps.tile([P, S], F32, name=f"hidden{t}", tag=f"shared{t}") for t in range(PACK)]
        h_rows = [sb.tile([P, S], F32, name=f"h_rows{t}") for t in range(PACK)]

        def fetch_a(u, far):
            cols = slice(HALF * u, HALF * (u + 1))
            for t in range(PACK):
                nc.scalar.activation(far[:, t, :], a_rows[t][:].indirect(n1_list[:, 8 * u : 8 * (u + 1)]), ACT.Copy)
                nc.vector.scalar_tensor_tensor(a_sum[u][:, t, :], a_bank[t][:, cols], factor[:, t : t + 1], far[:, t, :], ALU.mult, ALU.add)

        def layer(lo, hi):
            width = hi - lo
            u = lo // HALF
            inside = slice(lo - HALF * u, hi - HALF * u)
            gate = sb.tile([P, PACK, width], F32, name=f"gate{lo}")
            nc.scalar.activation(gate[:], b_sum[:, u, :, inside], ACT.Sigmoid, scale=0.0625)
            z = sb.tile([P, width, PACK], BF16, name=f"z{lo}", align_bytes=64)
            nc.vector.tensor_tensor(
                z[:].rearrange("p (c i) t -> p c t i", i=4),
                a_sum[u][:, :, inside].rearrange("p t (c i) -> p c t i", i=4),
                gate[:].rearrange("p t (c i) -> p c t i", i=4),
                ALU.mult,
            )
            z_words = sb.tile([P, width], U32, name=f"z_words{lo}", align_bytes=64)
            z_scales = sb.tile([P, width], U8, name=f"z_scales{lo}", align_bytes=64)
            nc.vector.quantize_mx(z_words[:].bitcast(FP8X4), z_scales[:], z[:].rearrange("p c t -> p (c t)"))
            return lo, hi, z_words, z_scales

        def multiply(t, lo, hi, z_words, z_scales):
            rows = slice(P * t, P * (t + 1))
            nc.tensor.matmul_mx(hidden[t][:, lo:hi], lhsT=w_dealt[:, rows].bitcast(FP8X4), lhsT_scale=w_scales[:, rows], rhs=z_words[:].bitcast(FP8X4), rhs_scale=z_scales[:], start=True, stop=True)

        fetch_a(0, a_first[:])
        first = layer(*PIECES[0])
        for t in range(PACK):
            multiply(t, *first)
        fetch_a(1, b_sum[:, 0, :, :])
        later = [layer(lo, hi) for lo, hi in PIECES[1:]]
        nc.scalar.copy(h_rows[0][:, 0:HALF], hidden[0][:, 0:HALF])
        for t in range(PACK):
            for piece in later:
                multiply(t, *piece)
            start = HALF if t == 0 else 0
            nc.vector.tensor_copy(h_rows[t][:, start:S], hidden[t][:, start:S])

        y_rounded = sb.tile([P, S, PACK], BF16, name="y_rounded", align_bytes=64)
        out_rows = out_0.rearrange("(p t) j -> p t j", t=PACK)
        y_words = sb.tile([P, S], U32, name="y_words", align_bytes=64)
        y_scales = sb.tile([P, S], U8, name="y_scales", align_bytes=64)
        for t in range(PACK):
            pair = sb.tile([P, 2, W], F32, name=f"pair{t}")
            nc.scalar.activation(pair[:, 0, :], h_rows[t][:].indirect(n3_list[:]), ACT.Copy)
            nc.scalar.activation(pair[:, 1, :], h_rows[t][:].indirect(n4_list[:]), ACT.Copy)
            mixed = sb.tile([P, 2, W], F32, name=f"mixed{t}")
            nc.vector.tensor_tensor(mixed[:, 0, :], pair[:, 0, :], pair[:, 1, :], ALU.add)
            nc.vector.tensor_tensor(mixed[:, 1, :], pair[:, 0, :], pair[:, 1, :], ALU.subtract)
            y = sb.tile([P, S], F32, name=f"y{t}")
            nc.scalar.activation(y[:].indirect(n3_list[:]), mixed[:, 0, :], ACT.Copy, scale=0.75)
            nc.scalar.activation(y[:].indirect(n4_list[:]), mixed[:, 1, :], ACT.Copy)
            nc.sync.dma_start(out_rows[:, t, :], y[:])
            for u in range(2):
                nc.vector.tensor_copy(y_rounded[:, HALF * u : HALF * (u + 1), t], y[:, HALF * u : HALF * (u + 1)])

        for u in range(2):
            cols = slice(HALF * u, HALF * (u + 1))
            nc.vector.quantize_mx(y_words[:, cols].bitcast(FP8X4), y_scales[:, cols], y_rounded[:, cols, :].rearrange("p c t -> p (c t)"))
            nc.sync.dma_start(words_of(out_1)[:, cols], y_words[:, cols].bitcast(I32))
        for q in range(4):
            queue = nc.sync if q == 3 else nc.scalar
            queue.dma_start(out_2[0, 4 * q : 4 * q + 4, :].bitcast(I32), y_scales[:].bitcast(I32)[32 * q : 32 * q + 4, :])
